import numpy as np
import ml_dtypes


def mxq(x, axis, fmt="e4m3"):
    dtype, down = {"e4m3": (ml_dtypes.float8_e4m3fn, 7), "e5m2": (ml_dtypes.float8_e5m2, 14)}[fmt]
    v = np.moveaxis(np.asarray(x, np.float32).astype(ml_dtypes.bfloat16).astype(np.float64), axis, -1)
    blocks = v.reshape(v.shape[:-1] + (-1, 32))
    amax = np.abs(blocks).max(-1, keepdims=True)
    byte = np.maximum(np.where(amax > 0, np.frexp(amax)[1] - 1 + 127, 0) - down, 1)
    scale = np.exp2(byte - 127.0)
    codes = (blocks / scale).astype(np.float32).astype(dtype).astype(np.float64)
    return np.moveaxis((codes * scale).reshape(v.shape), -1, axis)


WIDE = False


def mx_kscale(k):
    if not WIDE:
        return np.ones(k)
    levels = np.array([10, -10, 5, -5, 0])
    if k % 512:
        return np.exp2(np.random.permutation(np.resize(levels, k // 32))).repeat(32)
    a = np.empty((k // 512, 16))
    for p in range(k // 512):
        a[p, :8] = np.random.permutation(np.resize(levels, 8))
        for g in range(8):
            far = levels[np.abs(levels - a[p, g]) >= 10]
            a[p, g + 8] = far[np.random.randint(len(far))]
    return np.exp2(a.ravel()).repeat(32)


def f64(x):
    return np.asarray(x).astype(np.float64)


def striped(idx):
    return np.tile(idx.reshape(-1, 16).T, (8, 1)).astype(np.uint16)


def unstriped(offs):
    return offs[:16].T.reshape(-1).astype(np.int64)


def striped8(idx):
    return np.concatenate([x.reshape(-1, 16).T for x in idx]).astype(np.uint16)


def runs(offs, k):
    lists = np.stack([offs[16 * r : 16 * r + 16].T.reshape(-1) for r in range(8)]).astype(np.int64)
    return lists[np.arange(k) % 512 // 64]


def pack_weight(w):
    k, n = w.shape
    w = f64(np.asarray(w, np.float32).astype(ml_dtypes.bfloat16)).reshape(k // 32, 32, n)
    amax = np.abs(w).max(1)
    byte = np.clip(np.where(amax > 0, np.frexp(amax)[1] - 1 + 127 - 7, 1), 1, 254)
    scaled = (w * np.exp2(127.0 - byte)[:, None, :]).reshape(k, n).astype(np.float32)
    words = np.ascontiguousarray(scaled.reshape(k // 512, 128, 4, n).transpose(0, 1, 3, 2)).astype(ml_dtypes.float8_e4m3fn).view(np.uint8)
    return words, np.ascontiguousarray(byte.astype(np.uint8).reshape(k // 512, 16, n))


def unpack_weight(words, scales):
    g, p, n, _ = words.shape
    vals = np.ascontiguousarray(words).view(ml_dtypes.float8_e4m3fn).astype(np.float64) * np.repeat(np.exp2(scales.astype(np.float64) - 127.0), 8, axis=1)[..., None]
    return vals.transpose(0, 1, 3, 2).reshape(g * 512, n)


E2M1 = np.array([0.0, 0.5, 1.0, 1.5, 2.0, 3.0, 4.0, 6.0, -0.0, -0.5, -1.0, -1.5, -2.0, -3.0, -4.0, -6.0])


def pack_fp4(w):
    k, n = w.shape
    w = f64(np.asarray(w, np.float32).astype(ml_dtypes.bfloat16)).reshape(k // 32, 32, n)
    amax = np.abs(w).max(1)
    mant, ex = np.frexp(amax / 6.0)
    byte = np.clip(np.where(amax > 0, np.where(mant > 0.5, ex, ex - 1) + 127, 1), 1, 254)
    scaled = (w * np.exp2(127.0 - byte)[:, None, :]).reshape(k, n).astype(np.float32)
    c = np.ascontiguousarray(scaled.reshape(k // 512, 128, 4, n).transpose(0, 1, 3, 2)).astype(ml_dtypes.float4_e2m1fn).view(np.uint8) & 0xF
    words = (c[..., 0::2] | (c[..., 1::2] << 4)).reshape(k // 512, 128, 2 * n)
    return np.ascontiguousarray(words), np.ascontiguousarray(byte.astype(np.uint8).reshape(k // 512, 16, n))


def unpack_fp4(words, scales):
    g, _, n = scales.shape
    words = np.ascontiguousarray(words).reshape(g, 128, n, 2)
    nib = np.empty((g, 128, n, 4), np.uint8)
    nib[..., 0::2] = words & 0xF
    nib[..., 1::2] = words >> 4
    vals = E2M1[nib] * np.repeat(np.exp2(scales.astype(np.float64) - 127.0), 8, axis=1)[..., None]
    return vals.transpose(0, 1, 3, 2).reshape(g * 512, n)


def sigmoid(v):
    return 1.0 / (1.0 + np.exp(-np.maximum(v, -700.0)))

def planes(y):
    n, m = y.shape
    v = y.astype(np.float32).astype(ml_dtypes.bfloat16).astype(np.float64).reshape(n // 32, 32, m)
    top = np.abs(v).max(1)
    byte = np.clip(np.where(top > 0, np.frexp(top)[1] - 1 + 127 - 7, 1), 1, 254)
    codes = (v * np.exp2(127.0 - byte)[:, None, :]).reshape(n, m).astype(np.float32).astype(ml_dtypes.float8_e4m3fn).view(np.uint8)
    words = codes.reshape(n // 512, 128, 4, m).transpose(0, 1, 3, 2)
    return np.ascontiguousarray(words), np.ascontiguousarray(byte.astype(np.uint8).reshape(n // 512, 16, m))


K, T, S, V, H = 512, 2048, 512, 512, 512


def setup_inputs():
    n = np.random.standard_normal
    s = mx_kscale(K)[:, None]
    u = mx_kscale(S)
    packed_xT = pack_weight(n((K, T)) * s)
    packed_w1 = pack_fp4(n((K, H)) / np.sqrt(K) / s)
    packed_w2 = pack_fp4(n((K, H)) / np.sqrt(K) / s)
    return {
        "x_words": packed_xT[0],
        "x_scales": packed_xT[1],
        "w1_words": packed_w1[0],
        "w1_scales": packed_w1[1],
        "w2_words": packed_w2[0],
        "w2_scales": packed_w2[1],
        "ga": (np.random.uniform(0.5, 1.5, (H, 1)) * u[:, None]).astype(np.float32),
        "gb": (np.random.uniform(0.5, 1.5, (H, 1)) / u[:, None]).astype(np.float32),
        "offs": striped(np.random.permutation(T)[:S]),
        "two": striped(np.random.permutation(T)[:V]),
        "n1": striped8(np.stack([np.random.permutation(S) for _ in range(8)])),
        "n2": striped8(np.stack([np.random.permutation(S) for _ in range(8)])),
        "n3": striped8(np.stack([np.random.permutation(V) for _ in range(8)])),
        "n4": striped8(np.stack([np.random.permutation(V) for _ in range(8)])),
        "n5": striped8(np.stack([np.random.permutation(V) for _ in range(8)])),
    }


def reference(x_words, x_scales, w1_words, w1_scales, w2_words, w2_scales, ga, gb, offs, two, n1, n2, n3, n4, n5):
    xq = unpack_weight(x_words, x_scales)[:, unstriped(offs)]
    a = unpack_fp4(w1_words, w1_scales).T @ xq
    z = f64(ga) * ((a[np.arange(H)[:, None], runs(n1, H)]) / (np.abs(a) + np.abs(a[np.arange(H)[:, None], runs(n2, H)]) + 0.5))
    x_two = unpack_weight(x_words, x_scales)[:, unstriped(two)]
    b = unpack_fp4(w2_words, w2_scales).T @ x_two
    z2 = f64(gb) * (b * (sigmoid(b[np.arange(H)[:, None], runs(n3, H)])))
    s = 0.0625 * ((mxq(z, 0, "e4m3").T @ mxq(z2, 0, "e4m3")))
    st = s + s[np.arange(S)[:, None], runs(n4, S)]
    out_0 = st * (np.tanh(st[np.arange(S)[:, None], runs(n5, S)]))
    return (out_0,) + planes(out_0)

@@ -1,0 +1,228 @@
+from contextlib import ExitStack
+
+import concourse.mybir as mybir
+from concourse.masks import make_identity
+
+F32 = mybir.dt.float32
+BF16 = mybir.dt.bfloat16
+I32 = mybir.dt.int32
+U32 = mybir.dt.uint32
+U16 = mybir.dt.uint16
+U8 = mybir.dt.uint8
+FP8X4 = mybir.dt.float8_e4m3fn_x4
+FP4X4 = mybir.dt.float4_e2m1fn_x4
+ACT = mybir.ActivationFunctionType
+MULT = mybir.AluOpType.mult
+ADD = mybir.AluOpType.add
+
+P = 128
+T = 2048
+N = 512
+HALF = 256
+OUT_CHUNKS = ((0, 256), (256, 128), (384, 128))
+FLOPS = 3 * 2 * 512 * 512 * 512
+
+
+def tile_picked_kqnorm2gatehopp_none_po_kernel(tc, x_words, x_scales, w1_words, w1_scales, w2_words, w2_scales, ga, gb,
+        offs, two, n1, n2, n3, n4, n5, out_0, out_1, out_2):
+    nc = tc.nc
+    with ExitStack() as ctx:
+        sb = ctx.enter_context(tc.tile_pool(name="sb", bufs=1))
+        ps = ctx.enter_context(tc.psum_pool(name="ps", bufs=1))
+
+        def new_tile(name, shape, dtype, tag=None):
+            return sb.tile(shape, dtype, name=name, tag=tag or name, align_bytes=64)
+
+        def bank(name, tag, width=N):
+            return ps.tile([P, width], F32, name=name, tag=tag)
+
+        def load_list(name, src):
+            lst = new_tile(name, [P, N // 16], U16)
+            nc.sync.dma_start(lst[:], src)
+            return lst
+
+        def load_scale_rows(queue, plane, src):
+            for q in range(4):
+                queue.dma_start(plane[32 * q : 32 * q + 4, :].bitcast(I32), src[0, 4 * q : 4 * q + 4, :].bitcast(I32))
+
+        xs_raw = new_tile("xs_raw", [P, T], U8)
+        load_scale_rows(nc.sync, xs_raw, x_scales)
+        xw = new_tile("xw", [P, T], U32)
+        nc.sync.dma_start(xw[:].bitcast(I32), x_words[0].rearrange("p n t -> p (n t)").bitcast(I32))
+        l_offs = load_list("l_offs", offs)
+        w1w_raw = new_tile("w1w_raw", [P, 2 * N], U8)
+        w2w_raw = new_tile("w2w_raw", [P, 2 * N], U8)
+        nc.sync.dma_start(w1w_raw[:].bitcast(I32), w1_words[0].bitcast(I32))
+
+        four = new_tile("four", [P, 1], F32)
+        nc.vector.memset(four[:], 4.0)
+        half = new_tile("half", [P, 1], F32)
+        nc.scalar.activation(half[:], four[:], ACT.Abs_reciprocal_sqrt)
+        w1s_raw = new_tile("w1s_raw", [P, N], U8)
+        w2s_raw = new_tile("w2s_raw", [P, N], U8)
+        nc.vector.memset(w1s_raw[:].bitcast(I32), 0)
+        xs = new_tile("xs", [P, T], U8)
+        nc.vector.memset(xs[:].bitcast(I32), 0)
+        nc.vector.memset(w2s_raw[:].bitcast(I32), 0)
+        gain_rows = new_tile("gain_rows", [P, P], F32)
+        nc.vector.memset(gain_rows[:], 0.0)
+
+        load_scale_rows(nc.sync, w1s_raw, w1_scales)
+        l_two = load_list("l_two", two)
+        l_n2 = load_list("l_n2", n2)
+        nc.sync.dma_start(w2w_raw[:].bitcast(I32), w2_words[0].bitcast(I32))
+        load_scale_rows(nc.sync, w2s_raw, w2_scales)
+        for row, gain in ((0, ga), (4, gb)):
+            nc.sync.dma_start(
+                gain_rows[row : row + 4, :].rearrange("t (b i) -> t b i", i=8),
+                gain.rearrange("(b t i) o -> t b (i o)", t=4, i=8),
+            )
+        l_n1 = load_list("l_n1", n1)
+        l_n3 = load_list("l_n3", n3)
+        l_n4 = load_list("l_n4", n4)
+        l_n5 = load_list("l_n5", n5)
+        ident = new_tile("ident", [P, P], F32)
+        make_identity(nc, ident[:])
+        for q in range(4):
+            rows = slice(32 * q, 32 * q + 4)
+            nc.vector.tensor_copy(xs[rows, :].bitcast(I32), xs_raw[rows, :].bitcast(I32))
+
+        def deal(name, raw, width):
+            dealt = new_tile(name, [P, width], U8)
+            nc.vector.tensor_copy(
+                dealt[:].bitcast(I32).rearrange("p (t b w) -> p t b w", t=4, b=16),
+                raw[:].bitcast(I32).rearrange("p (b t w) -> p t b w", t=4, b=16),
+            )
+            return dealt
+
+        def pick(name, window, lst, dtype):
+            picked = new_tile(name, [P, N], dtype)
+            nc.vector.tensor_copy(picked[:], window[:].indirect(lst[:]))
+            return picked
+
+        def project(prefix, ww, ws, words, scales):
+            banks = []
+            for t in range(4):
+                acc = bank(f"{prefix}_acc{t}", f"{prefix}{t}")
+                nc.tensor.matmul_mx(
+                    out=acc[:],
+                    lhsT=ww[:, 2 * P * t : 2 * P * (t + 1)].bitcast(FP4X4),
+                    lhsT_scale=ws[:, P * t : P * (t + 1)],
+                    rhs=words[:].bitcast(FP8X4),
+                    rhs_scale=scales[:],
+                    start=True,
+                    stop=True,
+                )
+                banks.append(acc)
+            return banks
+
+        xa_s = pick("xa_s", xs, l_offs, U8)
+        w1w = deal("w1w", w1w_raw, 2 * N)
+        w1s = deal("w1s", w1s_raw, N)
+        xa_w = pick("xa_w", xw, l_offs, U32)
+        a_banks = project("a", w1w, w1s, xa_w, xa_s)
+        gain_bank = bank("gain_bank", "b3", P)
+        nc.tensor.transpose(gain_bank[:], gain_rows[:], ident[:])
+        gains = new_tile("gains", [P, 8], F32)
+        nc.vector.tensor_copy(gains[:], gain_bank[:, 0:8])
+        xb_s = pick("xb_s", xs, l_two, U8)
+        w2w = deal("w2w", w2w_raw, 2 * N)
+        w2s = deal("w2s", w2s_raw, N)
+        xb_w = pick("xb_w", xw, l_two, U32)
+        b_banks = project("b", w2w, w2s, xb_w, xb_s)
+
+        den = new_tile("den", [P, 4, N], F32, tag="den_then_sig")
+        for t in range(4):
+            size = new_tile(f"size{t}", [P, 2 * N], F32)
+            size2 = new_tile(f"size_again{t}", [P, N], F32)
+            nc.scalar.activation(size[:, 0:N], a_banks[t][:], ACT.Abs)
+            nc.scalar.activation(size2[:], a_banks[t][:], ACT.Abs)
+            nc.vector.tensor_tensor(den[:, t, :], size[:].indirect(l_n2[:]), size2[:], ADD)
+        root = new_tile("root", [P, 4, N], F32)
+        part = new_tile("part", [P, 4, N], F32)
+        for t in range(4):
+            ga_a = new_tile(f"ga_a{t}", [P, 2 * N], F32)
+            nc.scalar.activation(root[:, t, :], den[:, t, :], ACT.Abs_reciprocal_sqrt, bias=half[:])
+            nc.scalar.activation(ga_a[:, 0:N], a_banks[t][:], ACT.Copy, scale=gains[:, t : t + 1])
+            nc.vector.tensor_tensor(part[:, t, :], ga_a[:].indirect(l_n1[:]), root[:, t, :], MULT)
+        b_rows = []
+        for t in range(4):
+            b_t = new_tile(f"b_row{t}", [P, N], F32)
+            nc.scalar.activation(b_t[:], b_banks[t][:], ACT.Copy)
+            b_rows.append(b_t)
+        z_bf = new_tile("z_bf", [P, 4 * N], BF16)
+        nc.vector.tensor_tensor(
+            z_bf[:].rearrange("p (i c t) -> p c t i", i=4, t=4),
+            part[:].rearrange("p t (c i) -> p c t i", i=4),
+            root[:].rearrange("p t (c i) -> p c t i", i=4),
+            MULT,
+        )
+        z_w = new_tile("z_w", [P, N], U32)
+        z_s = new_tile("z_s", [P, N], U8)
+        nc.vector.quantize_mx(out=z_w[:].bitcast(FP8X4), scales=z_s[:], in_=z_bf[:])
+
+        sig = new_tile("sig", [P, 2, 4, HALF], F32, tag="den_then_sig")
+        s_banks = [bank(f"s_acc{t}", f"a{t}") for t in range(4)]
+        s_win = [new_tile(f"s_win{t}", [P, 2 * N], F32) for t in range(4)]
+        s_own = [new_tile(f"s_own{t}", [P, N], F32) for t in range(4)]
+        for h in range(2):
+            cols = slice(HALF * h, HALF * (h + 1))
+            z2 = new_tile(f"z2_{h}", [P, 4, HALF], F32)
+            for t in range(4):
+                nc.scalar.activation(sig[:, h, t, :], b_rows[t][:].indirect(l_n3[:, 16 * h : 16 * (h + 1)]), ACT.Sigmoid)
+                nc.vector.scalar_tensor_tensor(
+                    z2[:, t, :], b_banks[t][:, cols], gains[:, 4 + t : 5 + t], sig[:, h, t, :], MULT, MULT
+                )
+            z2_bf = new_tile(f"z2_bf{h}", [P, 4 * HALF], BF16)
+            nc.vector.tensor_copy(
+                z2_bf[:].rearrange("p (c i t) -> p c t i", i=4, t=4), z2[:].rearrange("p t (c i) -> p c t i", i=4)
+            )
+            z2_w = new_tile(f"z2_w{h}", [P, HALF], U32)
+            z2_s = new_tile(f"z2_s{h}", [P, HALF], U8)
+            nc.vector.quantize_mx(out=z2_w[:].bitcast(FP8X4), scales=z2_s[:], in_=z2_bf[:])
+            for t in range(4):
+                nc.tensor.matmul_mx(
+                    out=s_banks[t][:, cols],
+                    lhsT=z_w[:, P * t : P * (t + 1)].bitcast(FP8X4),
+                    lhsT_scale=z_s[:, P * t : P * (t + 1)],
+                    rhs=z2_w[:].bitcast(FP8X4),
+                    rhs_scale=z2_s[:],
+                    start=True,
+                    stop=True,
+                )
+                nc.scalar.activation(s_win[t][:, cols], s_banks[t][:, cols], ACT.Copy, scale=0.0625)
+                nc.scalar.activation(s_own[t][:, cols], s_banks[t][:, cols], ACT.Copy, scale=0.0625)
+
+        st, gate = [], []
+        for t in range(4):
+            st_t = new_tile(f"st{t}", [P, N], F32)
+            gate_t = new_tile(f"gate{t}", [P, N], F32)
+            nc.vector.tensor_tensor(st_t[:], s_win[t][:].indirect(l_n4[:]), s_own[t][:], ADD)
+            nc.scalar.activation(gate_t[:], st_t[:], ACT.Tanh)
+            st.append(st_t)
+            gate.append(gate_t)
+
+        out_rows = out_0.rearrange("(p t) v -> p t v", t=4)
+        out_words = out_1[0].rearrange("p n t -> p (n t)").bitcast(I32)
+        y_w = new_tile("y_w", [P, N], U32)
+        y_s = new_tile("y_s", [P, N], U8)
+        for c, (c0, width) in enumerate(OUT_CHUNKS):
+            cols = slice(c0, c0 + width)
+            y = new_tile(f"y{c}", [P, 4, width], F32)
+            for t in range(4):
+                nc.vector.tensor_tensor(
+                    y[:, t, :], gate[t][:].indirect(l_n5[:, c0 // 16 : (c0 + width) // 16]), st[t][:, cols], MULT
+                )
+            nc.sync.dma_start(out_rows[:, :, cols], y[:])
+            y_bf = new_tile(f"y_bf{c}", [P, 4 * width], BF16)
+            weave_out = y_bf[:].rearrange("p (c i t) -> p c t i", i=4, t=4)
+            weave_in = y[:].rearrange("p t (c i) -> p c t i", i=4)
+            if c < len(OUT_CHUNKS) - 1:
+                nc.scalar.copy(weave_out, weave_in)
+            else:
+                nc.vector.tensor_copy(weave_out, weave_in)
+            nc.vector.quantize_mx(out=y_w[:, cols].bitcast(FP8X4), scales=y_s[:, cols], in_=y_bf[:])
+            nc.sync.dma_start(out_words[:, cols], y_w[:, cols].bitcast(I32))
+        for q in range(4):
+            queue = nc.scalar if q % 2 else nc.sync
+            queue.dma_start(out_2[0, 4 * q : 4 * q + 4, :].bitcast(I32), y_s[32 * q : 32 * q + 4, :].bitcast(I32))

@@ -45,15 +45,8 @@ def tile_picked_kqnorm2gatehopp_none_po_kernel(tc, x_words, x_scales, w1_words, 
             for q in range(4):
                 queue.dma_start(plane[32 * q : 32 * q + 4, :].bitcast(I32), src[0, 4 * q : 4 * q + 4, :].bitcast(I32))
 
-        xs_raw = new_tile("xs_raw", [P, T], U8)
-        load_scale_rows(nc.sync, xs_raw, x_scales)
-        xw = new_tile("xw", [P, T], U32)
-        nc.sync.dma_start(xw[:].bitcast(I32), x_words[0].rearrange("p n t -> p (n t)").bitcast(I32))
-        l_offs = load_list("l_offs", offs)
-        w1w_raw = new_tile("w1w_raw", [P, 2 * N], U8)
-        w2w_raw = new_tile("w2w_raw", [P, 2 * N], U8)
-        nc.sync.dma_start(w1w_raw[:].bitcast(I32), w1_words[0].bitcast(I32))
-
+        xs = new_tile("xs", [P, T], U8)
+        nc.gpsimd.memset(xs[:].bitcast(I32), 0)
         four = new_tile("four", [P, 1], F32)
         nc.vector.memset(four[:], 4.0)
         half = new_tile("half", [P, 1], F32)
@@ -61,19 +54,24 @@ def tile_picked_kqnorm2gatehopp_none_po_kernel(tc, x_words, x_scales, w1_words, 
         w1s_raw = new_tile("w1s_raw", [P, N], U8)
         w2s_raw = new_tile("w2s_raw", [P, N], U8)
         nc.vector.memset(w1s_raw[:].bitcast(I32), 0)
-        xs = new_tile("xs", [P, T], U8)
-        nc.vector.memset(xs[:].bitcast(I32), 0)
         nc.vector.memset(w2s_raw[:].bitcast(I32), 0)
         gain_rows = new_tile("gain_rows", [P, P], F32)
         nc.vector.memset(gain_rows[:], 0.0)
 
-        load_scale_rows(nc.sync, w1s_raw, w1_scales)
+        l_offs = load_list("l_offs", offs)
         l_two = load_list("l_two", two)
+        load_scale_rows(nc.sync, xs, x_scales)
+        xw = new_tile("xw", [P, T], U32)
+        nc.sync.dma_start(xw[:].bitcast(I32), x_words[0].rearrange("p n t -> p (n t)").bitcast(I32))
+        w1w_raw = new_tile("w1w_raw", [P, 2 * N], U8)
+        w2w_raw = new_tile("w2w_raw", [P, 2 * N], U8)
+        nc.sync.dma_start(w1w_raw[:].bitcast(I32), w1_words[0].bitcast(I32))
+        load_scale_rows(nc.sync, w1s_raw, w1_scales)
         l_n2 = load_list("l_n2", n2)
         nc.sync.dma_start(w2w_raw[:].bitcast(I32), w2_words[0].bitcast(I32))
         load_scale_rows(nc.sync, w2s_raw, w2_scales)
         for row, gain in ((0, ga), (4, gb)):
-            nc.sync.dma_start(
+            nc.gpsimd.dma_start(
                 gain_rows[row : row + 4, :].rearrange("t (b i) -> t b i", i=8),
                 gain.rearrange("(b t i) o -> t b (i o)", t=4, i=8),
             )
@@ -83,10 +81,10 @@ def tile_picked_kqnorm2gatehopp_none_po_kernel(tc, x_words, x_scales, w1_words, 
         l_n5 = load_list("l_n5", n5)
         ident = new_tile("ident", [P, P], F32)
         make_identity(nc, ident[:])
-        for q in range(4):
-            rows = slice(32 * q, 32 * q + 4)
-            nc.vector.tensor_copy(xs[rows, :].bitcast(I32), xs_raw[rows, :].bitcast(I32))
-
+        gain_bank = bank("gain_bank", "b3", P)
+        nc.tensor.transpose(gain_bank[:], gain_rows[:], ident[:])
+        gains = new_tile("gains", [P, 8], F32)
+        nc.scalar.copy(gains[:], gain_bank[:, 0:8])
         def deal(name, raw, width):
             dealt = new_tile(name, [P, width], U8)
             nc.vector.tensor_copy(
@@ -95,8 +93,8 @@ def tile_picked_kqnorm2gatehopp_none_po_kernel(tc, x_words, x_scales, w1_words, 
             )
             return dealt
 
-        def pick(name, window, lst, dtype):
-            picked = new_tile(name, [P, N], dtype)
+        def pick(name, window, lst, dtype, tag=None):
+            picked = new_tile(name, [P, N], dtype, tag)
             nc.vector.tensor_copy(picked[:], window[:].indirect(lst[:]))
             return picked
 
@@ -117,18 +115,15 @@ def tile_picked_kqnorm2gatehopp_none_po_kernel(tc, x_words, x_scales, w1_words, 
             return banks
 
         xa_s = pick("xa_s", xs, l_offs, U8)
+        xa_w = pick("xa_w", xw, l_offs, U32)
         w1w = deal("w1w", w1w_raw, 2 * N)
         w1s = deal("w1s", w1s_raw, N)
-        xa_w = pick("xa_w", xw, l_offs, U32)
         a_banks = project("a", w1w, w1s, xa_w, xa_s)
-        gain_bank = bank("gain_bank", "b3", P)
-        nc.tensor.transpose(gain_bank[:], gain_rows[:], ident[:])
-        gains = new_tile("gains", [P, 8], F32)
-        nc.vector.tensor_copy(gains[:], gain_bank[:, 0:8])
         xb_s = pick("xb_s", xs, l_two, U8)
+        xb_w = pick("xb_w", xw, l_two, U32, "w1s_raw")
+
         w2w = deal("w2w", w2w_raw, 2 * N)
         w2s = deal("w2s", w2s_raw, N)
-        xb_w = pick("xb_w", xw, l_two, U32)
         b_banks = project("b", w2w, w2s, xb_w, xb_s)
 
         den = new_tile("den", [P, 4, N], F32, tag="den_then_sig")
@@ -136,35 +131,42 @@ def tile_picked_kqnorm2gatehopp_none_po_kernel(tc, x_words, x_scales, w1_words, 
             size = new_tile(f"size{t}", [P, 2 * N], F32)
             size2 = new_tile(f"size_again{t}", [P, N], F32)
             nc.scalar.activation(size[:, 0:N], a_banks[t][:], ACT.Abs)
-            nc.scalar.activation(size2[:], a_banks[t][:], ACT.Abs)
+            nc.vector.tensor_copy(size2[:], size[:, 0:N])
             nc.vector.tensor_tensor(den[:, t, :], size[:].indirect(l_n2[:]), size2[:], ADD)
+
+
         root = new_tile("root", [P, 4, N], F32)
         part = new_tile("part", [P, 4, N], F32)
-        for t in range(4):
-            ga_a = new_tile(f"ga_a{t}", [P, 2 * N], F32)
-            nc.scalar.activation(root[:, t, :], den[:, t, :], ACT.Abs_reciprocal_sqrt, bias=half[:])
-            nc.scalar.activation(ga_a[:, 0:N], a_banks[t][:], ACT.Copy, scale=gains[:, t : t + 1])
-            nc.vector.tensor_tensor(part[:, t, :], ga_a[:].indirect(l_n1[:]), root[:, t, :], MULT)
         b_rows = []
         for t in range(4):
+            ga_a = new_tile(f"ga_a{t}", [P, 2 * N], F32)
             b_t = new_tile(f"b_row{t}", [P, N], F32)
-            nc.scalar.activation(b_t[:], b_banks[t][:], ACT.Copy)
+            nc.scalar.activation(ga_a[:, 0:N], a_banks[t][:], ACT.Copy, scale=gains[:, t : t + 1])
+            nc.scalar.activation(root[:, t, :], den[:, t, :], ACT.Abs_reciprocal_sqrt, bias=half[:])
+            nc.vector.tensor_tensor(part[:, t, :], ga_a[:].indirect(l_n1[:]), root[:, t, :], MULT)
+            if t == 0:
+                nc.vector.tensor_copy(b_t[:], b_banks[t][:])
+            else:
+                nc.scalar.activation(b_t[:], b_banks[t][:], ACT.Copy)
             b_rows.append(b_t)
-        z_bf = new_tile("z_bf", [P, 4 * N], BF16)
-        nc.vector.tensor_tensor(
-            z_bf[:].rearrange("p (i c t) -> p c t i", i=4, t=4),
-            part[:].rearrange("p t (c i) -> p c t i", i=4),
-            root[:].rearrange("p t (c i) -> p c t i", i=4),
-            MULT,
-        )
-        z_w = new_tile("z_w", [P, N], U32)
-        z_s = new_tile("z_s", [P, N], U8)
-        nc.vector.quantize_mx(out=z_w[:].bitcast(FP8X4), scales=z_s[:], in_=z_bf[:])
+
+        def quantise_z(u, tag):
+            z_bf = new_tile(f"z_bf{u}", [P, 2 * N], BF16, tag)
+            nc.vector.tensor_tensor(
+                z_bf[:].rearrange("p (i c t) -> p c t i", i=2, t=4),
+                part[:].rearrange("p t (c i) -> p c t i", i=4)[:, :, :, 2 * u : 2 * u + 2],
+                root[:].rearrange("p t (c i) -> p c t i", i=4)[:, :, :, 2 * u : 2 * u + 2],
+                MULT,
+            )
+            z_w = new_tile(f"z_w{u}", [P, HALF], U32)
+            z_s = new_tile(f"z_s{u}", [P, HALF], U8)
+            nc.vector.quantize_mx(out=z_w[:].bitcast(FP8X4), scales=z_s[:], in_=z_bf[:])
+            return z_w, z_s
+
+        z_planes = [quantise_z(0, None)]
 
         sig = new_tile("sig", [P, 2, 4, HALF], F32, tag="den_then_sig")
-        s_banks = [bank(f"s_acc{t}", f"a{t}") for t in range(4)]
-        s_win = [new_tile(f"s_win{t}", [P, 2 * N], F32) for t in range(4)]
-        s_own = [new_tile(f"s_own{t}", [P, N], F32) for t in range(4)]
+        z2_planes = []
         for h in range(2):
             cols = slice(HALF * h, HALF * (h + 1))
             z2 = new_tile(f"z2_{h}", [P, 4, HALF], F32)
@@ -180,48 +182,69 @@ def tile_picked_kqnorm2gatehopp_none_po_kernel(tc, x_words, x_scales, w1_words, 
             z2_w = new_tile(f"z2_w{h}", [P, HALF], U32)
             z2_s = new_tile(f"z2_s{h}", [P, HALF], U8)
             nc.vector.quantize_mx(out=z2_w[:].bitcast(FP8X4), scales=z2_s[:], in_=z2_bf[:])
+            z2_planes.append((z2_w, z2_s))
+
+        z_planes.append(quantise_z(1, "z2_bf1"))
+
+        s_banks = [bank(f"s_acc{t}", f"a{t}") for t in range(4)]
+        s_win = [new_tile(f"s_win{t}", [P, 2 * N], F32) for t in range(4)]
+        s_own = [new_tile(f"s_own{t}", [P, N], F32) for t in range(4)]
+
+        def empty_bank(t, cols):
+            nc.scalar.activation(s_win[t][:, cols], s_banks[t][:, cols], ACT.Copy, scale=0.0625)
+            nc.scalar.activation(s_own[t][:, cols], s_banks[t][:, cols], ACT.Copy, scale=0.0625)
+
+        for h, (z2_w, z2_s) in enumerate(z2_planes):
+            cols = slice(HALF * h, HALF * (h + 1))
             for t in range(4):
+                z_w, z_s = z_planes[t // 2]
+                rows = slice(P * (t % 2), P * (t % 2 + 1))
                 nc.tensor.matmul_mx(
                     out=s_banks[t][:, cols],
-                    lhsT=z_w[:, P * t : P * (t + 1)].bitcast(FP8X4),
-                    lhsT_scale=z_s[:, P * t : P * (t + 1)],
+                    lhsT=z_w[:, rows].bitcast(FP8X4),
+                    lhsT_scale=z_s[:, rows],
                     rhs=z2_w[:].bitcast(FP8X4),
                     rhs_scale=z2_s[:],
                     start=True,
                     stop=True,
                 )
-                nc.scalar.activation(s_win[t][:, cols], s_banks[t][:, cols], ACT.Copy, scale=0.0625)
-                nc.scalar.activation(s_own[t][:, cols], s_banks[t][:, cols], ACT.Copy, scale=0.0625)
+                if t < 2:
+                    empty_bank(t, cols)
+                elif h == 1:
+                    empty_bank(t, slice(0, N))
 
         st, gate = [], []
         for t in range(4):
-            st_t = new_tile(f"st{t}", [P, N], F32)
-            gate_t = new_tile(f"gate{t}", [P, N], F32)
+            st_t = new_tile(f"st{t}", [P, N], F32, "z2_bf1" if t == 0 else None)
+            gate_t = new_tile(f"gate{t}", [P, 2 * N], F32)
             nc.vector.tensor_tensor(st_t[:], s_win[t][:].indirect(l_n4[:]), s_own[t][:], ADD)
-            nc.scalar.activation(gate_t[:], st_t[:], ACT.Tanh)
+            nc.scalar.activation(gate_t[:, 0:N], st_t[:], ACT.Tanh)
             st.append(st_t)
             gate.append(gate_t)
 
         out_rows = out_0.rearrange("(p t) v -> p t v", t=4)
         out_words = out_1[0].rearrange("p n t -> p (n t)").bitcast(I32)
+        y = new_tile("y", [P, 4, N], F32)
         y_w = new_tile("y_w", [P, N], U32)
         y_s = new_tile("y_s", [P, N], U8)
-        for c, (c0, width) in enumerate(OUT_CHUNKS):
-            cols = slice(c0, c0 + width)
-            y = new_tile(f"y{c}", [P, 4, width], F32)
-            for t in range(4):
-                nc.vector.tensor_tensor(
-                    y[:, t, :], gate[t][:].indirect(l_n5[:, c0 // 16 : (c0 + width) // 16]), st[t][:, cols], MULT
-                )
-            nc.sync.dma_start(out_rows[:, :, cols], y[:])
-            y_bf = new_tile(f"y_bf{c}", [P, 4 * width], BF16)
-            weave_out = y_bf[:].rearrange("p (c i t) -> p c t i", i=4, t=4)
-            weave_in = y[:].rearrange("p t (c i) -> p c t i", i=4)
-            if c < len(OUT_CHUNKS) - 1:
-                nc.scalar.copy(weave_out, weave_in)
-            else:
-                nc.vector.tensor_copy(weave_out, weave_in)
-            nc.vector.quantize_mx(out=y_w[:, cols].bitcast(FP8X4), scales=y_s[:, cols], in_=y_bf[:])
+        for t in range(3):
+            nc.vector.tensor_tensor(y[:, t, :], gate[t][:].indirect(l_n5[:]), st[t][:], MULT)
+            nc.sync.dma_start(out_rows[:, t, :], y[:, t, :])
+        halves = [slice(0, HALF), slice(HALF, N)]
+        for h, cols in enumerate(halves):
+            nc.vector.tensor_tensor(
+                y[:, 3, cols], gate[3][:].indirect(l_n5[:, 16 * h : 16 * (h + 1)]), st[3][:, cols], MULT
+            )
+        nc.sync.dma_start(out_rows[:, 3, :], y[:, 3, :])
+        y_bf = [new_tile(f"y_bf{h}", [P, 4 * HALF], BF16) for h in range(2)]
+        for h, weave in enumerate((nc.scalar.copy, nc.vector.tensor_copy)):
+            weave(
+                y_bf[h][:].rearrange("p (c i t) -> p c t i", i=4, t=4),
+                y[:, :, halves[h]].rearrange("p t (c i) -> p c t i", i=4),
+            )
+        for h in (1, 0):
+            cols = halves[h]
+            nc.vector.quantize_mx(out=y_w[:, cols].bitcast(FP8X4), scales=y_s[:, cols], in_=y_bf[h][:])
             nc.sync.dma_start(out_words[:, cols], y_w[:, cols].bitcast(I32))
         for q in range(4):
             queue = nc.scalar if q % 2 else nc.sync

@@ -98,9 +98,9 @@ def tile_picked_kqnorm2gatehopp_none_po_kernel(tc, x_words, x_scales, w1_words, 
             nc.vector.tensor_copy(picked[:], window[:].indirect(lst[:]))
             return picked
 
-        def project(prefix, ww, ws, words, scales):
-            banks = []
-            for t in range(4):
+        def project(prefix, ww, ws, words, scales, order):
+            banks = {}
+            for t in order:
                 acc = bank(f"{prefix}_acc{t}", f"{prefix}{t}")
                 nc.tensor.matmul_mx(
                     out=acc[:],
@@ -111,29 +111,32 @@ def tile_picked_kqnorm2gatehopp_none_po_kernel(tc, x_words, x_scales, w1_words, 
                     start=True,
                     stop=True,
                 )
-                banks.append(acc)
+                banks[t] = acc
             return banks
 
         xa_s = pick("xa_s", xs, l_offs, U8)
         xa_w = pick("xa_w", xw, l_offs, U32)
         w1w = deal("w1w", w1w_raw, 2 * N)
         w1s = deal("w1s", w1s_raw, N)
-        a_banks = project("a", w1w, w1s, xa_w, xa_s)
+        a_banks = project("a", w1w, w1s, xa_w, xa_s, (0, 2, 3, 1))
         xb_s = pick("xb_s", xs, l_two, U8)
         xb_w = pick("xb_w", xw, l_two, U32, "w1s_raw")
 
         w2w = deal("w2w", w2w_raw, 2 * N)
         w2s = deal("w2s", w2s_raw, N)
-        b_banks = project("b", w2w, w2s, xb_w, xb_s)
+        b_banks = project("b", w2w, w2s, xb_w, xb_s, (0, 1, 2, 3))
 
         den = new_tile("den", [P, 4, N], F32, tag="den_then_sig")
+        size = [new_tile(f"size{t}", [P, 2 * N], F32) for t in range(4)]
+        size2 = [new_tile(f"size_again{t}", [P, N], F32) for t in range(4)]
+        for t in (0, 2, 3, 1):
+            nc.scalar.activation(size[t][:, 0:N], a_banks[t][:], ACT.Abs)
+            if t >= 2:
+                nc.sync.dma_start(size2[t][:], size[t][:, 0:N])
         for t in range(4):
-            size = new_tile(f"size{t}", [P, 2 * N], F32)
-            size2 = new_tile(f"size_again{t}", [P, N], F32)
-            nc.scalar.activation(size[:, 0:N], a_banks[t][:], ACT.Abs)
-            nc.vector.tensor_copy(size2[:], size[:, 0:N])
-            nc.vector.tensor_tensor(den[:, t, :], size[:].indirect(l_n2[:]), size2[:], ADD)
-
+            if t < 2:
+                nc.vector.tensor_copy(size2[t][:], size[t][:, 0:N])
+            nc.vector.tensor_tensor(den[:, t, :], size[t][:].indirect(l_n2[:]), size2[t][:], ADD)
 
         root = new_tile("root", [P, 4, N], F32)
         part = new_tile("part", [P, 4, N], F32)
@@ -144,10 +147,7 @@ def tile_picked_kqnorm2gatehopp_none_po_kernel(tc, x_words, x_scales, w1_words, 
             nc.scalar.activation(ga_a[:, 0:N], a_banks[t][:], ACT.Copy, scale=gains[:, t : t + 1])
             nc.scalar.activation(root[:, t, :], den[:, t, :], ACT.Abs_reciprocal_sqrt, bias=half[:])
             nc.vector.tensor_tensor(part[:, t, :], ga_a[:].indirect(l_n1[:]), root[:, t, :], MULT)
-            if t == 0:
-                nc.vector.tensor_copy(b_t[:], b_banks[t][:])
-            else:
-                nc.scalar.activation(b_t[:], b_banks[t][:], ACT.Copy)
+            nc.scalar.activation(b_t[:], b_banks[t][:], ACT.Copy)
             b_rows.append(b_t)
 
         def quantise_z(u, tag):

from contextlib import ExitStack

import concourse.mybir as mybir
from concourse.masks import make_identity

F32 = mybir.dt.float32
BF16 = mybir.dt.bfloat16
I32 = mybir.dt.int32
U32 = mybir.dt.uint32
U16 = mybir.dt.uint16
U8 = mybir.dt.uint8
FP8X4 = mybir.dt.float8_e4m3fn_x4
FP4X4 = mybir.dt.float4_e2m1fn_x4
ACT = mybir.ActivationFunctionType
MULT = mybir.AluOpType.mult
ADD = mybir.AluOpType.add

P = 128
T = 2048
N = 512
HALF = 256
OUT_CHUNKS = ((0, 256), (256, 128), (384, 128))
FLOPS = 3 * 2 * 512 * 512 * 512


def tile_picked_kqnorm2gatehopp_none_po_kernel(tc, x_words, x_scales, w1_words, w1_scales, w2_words, w2_scales, ga, gb,
        offs, two, n1, n2, n3, n4, n5, out_0, out_1, out_2):
    nc = tc.nc
    with ExitStack() as ctx:
        sb = ctx.enter_context(tc.tile_pool(name="sb", bufs=1))
        ps = ctx.enter_context(tc.psum_pool(name="ps", bufs=1))

        def new_tile(name, shape, dtype, tag=None):
            return sb.tile(shape, dtype, name=name, tag=tag or name, align_bytes=64)

        def bank(name, tag, width=N):
            return ps.tile([P, width], F32, name=name, tag=tag)

        def load_list(name, src):
            lst = new_tile(name, [P, N // 16], U16)
            nc.sync.dma_start(lst[:], src)
            return lst

        def load_scale_rows(queue, plane, src):
            for q in range(4):
                queue.dma_start(plane[32 * q : 32 * q + 4, :].bitcast(I32), src[0, 4 * q : 4 * q + 4, :].bitcast(I32))

        xs = new_tile("xs", [P, T], U8)
        nc.gpsimd.memset(xs[:].bitcast(I32), 0)
        four = new_tile("four", [P, 1], F32)
        nc.vector.memset(four[:], 4.0)
        half = new_tile("half", [P, 1], F32)
        nc.scalar.activation(half[:], four[:], ACT.Abs_reciprocal_sqrt)
        w1s_raw = new_tile("w1s_raw", [P, N], U8)
        w2s_raw = new_tile("w2s_raw", [P, N], U8)
        nc.vector.memset(w1s_raw[:].bitcast(I32), 0)
        nc.vector.memset(w2s_raw[:].bitcast(I32), 0)
        gain_rows = new_tile("gain_rows", [P, P], F32)
        nc.vector.memset(gain_rows[:], 0.0)

        l_offs = load_list("l_offs", offs)
        l_two = load_list("l_two", two)
        load_scale_rows(nc.sync, xs, x_scales)
        xw = new_tile("xw", [P, T], U32)
        nc.sync.dma_start(xw[:].bitcast(I32), x_words[0].rearrange("p n t -> p (n t)").bitcast(I32))
        w1w_raw = new_tile("w1w_raw", [P, 2 * N], U8)
        w2w_raw = new_tile("w2w_raw", [P, 2 * N], U8)
        nc.sync.dma_start(w1w_raw[:].bitcast(I32), w1_words[0].bitcast(I32))
        load_scale_rows(nc.sync, w1s_raw, w1_scales)
        l_n2 = load_list("l_n2", n2)
        nc.sync.dma_start(w2w_raw[:].bitcast(I32), w2_words[0].bitcast(I32))
        load_scale_rows(nc.sync, w2s_raw, w2_scales)
        for row, gain in ((0, ga), (4, gb)):
            nc.gpsimd.dma_start(
                gain_rows[row : row + 4, :].rearrange("t (b i) -> t b i", i=8),
                gain.rearrange("(b t i) o -> t b (i o)", t=4, i=8),
            )
        l_n1 = load_list("l_n1", n1)
        l_n3 = load_list("l_n3", n3)
        l_n4 = load_list("l_n4", n4)
        l_n5 = load_list("l_n5", n5)
        ident = new_tile("ident", [P, P], F32)
        make_identity(nc, ident[:])
        gain_bank = bank("gain_bank", "b3", P)
        nc.tensor.transpose(gain_bank[:], gain_rows[:], ident[:])
        gains = new_tile("gains", [P, 8], F32)
        nc.scalar.copy(gains[:], gain_bank[:, 0:8])
        def deal(name, raw, width):
            dealt = new_tile(name, [P, width], U8)
            nc.vector.tensor_copy(
                dealt[:].bitcast(I32).rearrange("p (t b w) -> p t b w", t=4, b=16),
                raw[:].bitcast(I32).rearrange("p (b t w) -> p t b w", t=4, b=16),
            )
            return dealt

        def pick(name, window, lst, dtype, tag=None):
            picked = new_tile(name, [P, N], dtype, tag)
            nc.vector.tensor_copy(picked[:], window[:].indirect(lst[:]))
            return picked

        def project(prefix, ww, ws, words, scales, order):
            banks = {}
            for t in order:
                acc = bank(f"{prefix}_acc{t}", f"{prefix}{t}")
                nc.tensor.matmul_mx(
                    out=acc[:],
                    lhsT=ww[:, 2 * P * t : 2 * P * (t + 1)].bitcast(FP4X4),
                    lhsT_scale=ws[:, P * t : P * (t + 1)],
                    rhs=words[:].bitcast(FP8X4),
                    rhs_scale=scales[:],
                    start=True,
                    stop=True,
                )
                banks[t] = acc
            return banks

        xa_s = pick("xa_s", xs, l_offs, U8)
        xa_w = pick("xa_w", xw, l_offs, U32)
        w1w = deal("w1w", w1w_raw, 2 * N)
        w1s = deal("w1s", w1s_raw, N)
        a_banks = project("a", w1w, w1s, xa_w, xa_s, (0, 2, 3, 1))
        xb_s = pick("xb_s", xs, l_two, U8)
        xb_w = pick("xb_w", xw, l_two, U32, "w1s_raw")

        w2w = deal("w2w", w2w_raw, 2 * N)
        w2s = deal("w2s", w2s_raw, N)
        b_banks = project("b", w2w, w2s, xb_w, xb_s, (0, 1, 2, 3))

        den = new_tile("den", [P, 4, N], F32, tag="den_then_sig")
        size = [new_tile(f"size{t}", [P, 2 * N], F32) for t in range(4)]
        size2 = [new_tile(f"size_again{t}", [P, N], F32) for t in range(4)]
        for t in (0, 2, 3, 1):
            nc.scalar.activation(size[t][:, 0:N], a_banks[t][:], ACT.Abs)
            if t >= 2:
                nc.sync.dma_start(size2[t][:], size[t][:, 0:N])
        for t in range(4):
            if t < 2:
                nc.vector.tensor_copy(size2[t][:], size[t][:, 0:N])
            nc.vector.tensor_tensor(den[:, t, :], size[t][:].indirect(l_n2[:]), size2[t][:], ADD)

        root = new_tile("root", [P, 4, N], F32)
        part = new_tile("part", [P, 4, N], F32)
        b_rows = []
        for t in range(4):
            ga_a = new_tile(f"ga_a{t}", [P, 2 * N], F32)
            b_t = new_tile(f"b_row{t}", [P, N], F32)
            nc.scalar.activation(ga_a[:, 0:N], a_banks[t][:], ACT.Copy, scale=gains[:, t : t + 1])
            nc.scalar.activation(root[:, t, :], den[:, t, :], ACT.Abs_reciprocal_sqrt, bias=half[:])
            nc.vector.tensor_tensor(part[:, t, :], ga_a[:].indirect(l_n1[:]), root[:, t, :], MULT)
            nc.scalar.activation(b_t[:], b_banks[t][:], ACT.Copy)
            b_rows.append(b_t)

        def quantise_z(u, tag):
            z_bf = new_tile(f"z_bf{u}", [P, 2 * N], BF16, tag)
            nc.vector.tensor_tensor(
                z_bf[:].rearrange("p (i c t) -> p c t i", i=2, t=4),
                part[:].rearrange("p t (c i) -> p c t i", i=4)[:, :, :, 2 * u : 2 * u + 2],
                root[:].rearrange("p t (c i) -> p c t i", i=4)[:, :, :, 2 * u : 2 * u + 2],
                MULT,
            )
            z_w = new_tile(f"z_w{u}", [P, HALF], U32)
            z_s = new_tile(f"z_s{u}", [P, HALF], U8)
            nc.vector.quantize_mx(out=z_w[:].bitcast(FP8X4), scales=z_s[:], in_=z_bf[:])
            return z_w, z_s

        z_planes = [quantise_z(0, None)]

        sig = new_tile("sig", [P, 2, 4, HALF], F32, tag="den_then_sig")
        z2_planes = []
        for h in range(2):
            cols = slice(HALF * h, HALF * (h + 1))
            z2 = new_tile(f"z2_{h}", [P, 4, HALF], F32)
            for t in range(4):
                nc.scalar.activation(sig[:, h, t, :], b_rows[t][:].indirect(l_n3[:, 16 * h : 16 * (h + 1)]), ACT.Sigmoid)
                nc.vector.scalar_tensor_tensor(
                    z2[:, t, :], b_banks[t][:, cols], gains[:, 4 + t : 5 + t], sig[:, h, t, :], MULT, MULT
                )
            z2_bf = new_tile(f"z2_bf{h}", [P, 4 * HALF], BF16)
            nc.vector.tensor_copy(
                z2_bf[:].rearrange("p (c i t) -> p c t i", i=4, t=4), z2[:].rearrange("p t (c i) -> p c t i", i=4)
            )
            z2_w = new_tile(f"z2_w{h}", [P, HALF], U32)
            z2_s = new_tile(f"z2_s{h}", [P, HALF], U8)
            nc.vector.quantize_mx(out=z2_w[:].bitcast(FP8X4), scales=z2_s[:], in_=z2_bf[:])
            z2_planes.append((z2_w, z2_s))

        z_planes.append(quantise_z(1, "z2_bf1"))

        s_banks = [bank(f"s_acc{t}", f"a{t}") for t in range(4)]
        s_win = [new_tile(f"s_win{t}", [P, 2 * N], F32) for t in range(4)]
        s_own = [new_tile(f"s_own{t}", [P, N], F32) for t in range(4)]

        def empty_bank(t, cols):
            nc.scalar.activation(s_win[t][:, cols], s_banks[t][:, cols], ACT.Copy, scale=0.0625)
            nc.scalar.activation(s_own[t][:, cols], s_banks[t][:, cols], ACT.Copy, scale=0.0625)

        for h, (z2_w, z2_s) in enumerate(z2_planes):
            cols = slice(HALF * h, HALF * (h + 1))
            for t in range(4):
                z_w, z_s = z_planes[t // 2]
                rows = slice(P * (t % 2), P * (t % 2 + 1))
                nc.tensor.matmul_mx(
                    out=s_banks[t][:, cols],
                    lhsT=z_w[:, rows].bitcast(FP8X4),
                    lhsT_scale=z_s[:, rows],
                    rhs=z2_w[:].bitcast(FP8X4),
                    rhs_scale=z2_s[:],
                    start=True,
                    stop=True,
                )
                if t < 2:
                    empty_bank(t, cols)
                elif h == 1:
                    empty_bank(t, slice(0, N))

        st, gate = [], []
        for t in range(4):
            st_t = new_tile(f"st{t}", [P, N], F32, "z2_bf1" if t == 0 else None)
            gate_t = new_tile(f"gate{t}", [P, 2 * N], F32)
            nc.vector.tensor_tensor(st_t[:], s_win[t][:].indirect(l_n4[:]), s_own[t][:], ADD)
            nc.scalar.activation(gate_t[:, 0:N], st_t[:], ACT.Tanh)
            st.append(st_t)
            gate.append(gate_t)

        out_rows = out_0.rearrange("(p t) v -> p t v", t=4)
        out_words = out_1[0].rearrange("p n t -> p (n t)").bitcast(I32)
        y = new_tile("y", [P, 4, N], F32)
        y_w = new_tile("y_w", [P, N], U32)
        y_s = new_tile("y_s", [P, N], U8)
        for t in range(3):
            nc.vector.tensor_tensor(y[:, t, :], gate[t][:].indirect(l_n5[:]), st[t][:], MULT)
            nc.sync.dma_start(out_rows[:, t, :], y[:, t, :])
        halves = [slice(0, HALF), slice(HALF, N)]
        for h, cols in enumerate(halves):
            nc.vector.tensor_tensor(
                y[:, 3, cols], gate[3][:].indirect(l_n5[:, 16 * h : 16 * (h + 1)]), st[3][:, cols], MULT
            )
        nc.sync.dma_start(out_rows[:, 3, :], y[:, 3, :])
        y_bf = [new_tile(f"y_bf{h}", [P, 4 * HALF], BF16) for h in range(2)]
        for h, weave in enumerate((nc.scalar.copy, nc.vector.tensor_copy)):
            weave(
                y_bf[h][:].rearrange("p (c i t) -> p c t i", i=4, t=4),
                y[:, :, halves[h]].rearrange("p t (c i) -> p c t i", i=4),
            )
        for h in (1, 0):
            cols = halves[h]
            nc.vector.quantize_mx(out=y_w[:, cols].bitcast(FP8X4), scales=y_s[:, cols], in_=y_bf[h][:])
            nc.sync.dma_start(out_words[:, cols], y_w[:, cols].bitcast(I32))
        for q in range(4):
            queue = nc.scalar if q % 2 else nc.sync
            queue.dma_start(out_2[0, 4 * q : 4 * q + 4, :].bitcast(I32), y_s[32 * q : 32 * q + 4, :].bitcast(I32))
